import numpy as np
import ml_dtypes


def mxq(x, axis, fmt="e4m3"):
    dtype, down = {"e4m3": (ml_dtypes.float8_e4m3fn, 7), "e5m2": (ml_dtypes.float8_e5m2, 14)}[fmt]
    v = np.moveaxis(np.asarray(x, np.float32).astype(ml_dtypes.bfloat16).astype(np.float64), axis, -1)
    blocks = v.reshape(v.shape[:-1] + (-1, 32))
    amax = np.abs(blocks).max(-1, keepdims=True)
    byte = np.maximum(np.where(amax > 0, np.frexp(amax)[1] - 1 + 127, 0) - down, 1)
    scale = np.exp2(byte - 127.0)
    codes = (blocks / scale).astype(np.float32).astype(dtype).astype(np.float64)
    return np.moveaxis((codes * scale).reshape(v.shape), -1, axis)


WIDE = False


def mx_kscale(k):
    if not WIDE:
        return np.ones(k)
    levels = np.array([10, -10, 5, -5, 0])
    if k % 512:
        return np.exp2(np.random.permutation(np.resize(levels, k // 32))).repeat(32)
    a = np.empty((k // 512, 16))
    for p in range(k // 512):
        a[p, :8] = np.random.permutation(np.resize(levels, 8))
        for g in range(8):
            far = levels[np.abs(levels - a[p, g]) >= 10]
            a[p, g + 8] = far[np.random.randint(len(far))]
    return np.exp2(a.ravel()).repeat(32)


def f64(x):
    return np.asarray(x).astype(np.float64)


def striped8(idx):
    return np.concatenate([x.reshape(-1, 16).T for x in idx]).astype(np.uint16)


def runs(offs, k):
    lists = np.stack([offs[16 * r : 16 * r + 16].T.reshape(-1) for r in range(8)]).astype(np.int64)
    return lists[np.arange(k) % 512 // 64]


def pack_weight(w):
    k, n = w.shape
    w = f64(np.asarray(w, np.float32).astype(ml_dtypes.bfloat16)).reshape(k // 32, 32, n)
    amax = np.abs(w).max(1)
    byte = np.clip(np.where(amax > 0, np.frexp(amax)[1] - 1 + 127 - 7, 1), 1, 254)
    scaled = (w * np.exp2(127.0 - byte)[:, None, :]).reshape(k, n).astype(np.float32)
    words = np.ascontiguousarray(scaled.reshape(k // 512, 128, 4, n).transpose(0, 1, 3, 2)).astype(ml_dtypes.float8_e4m3fn).view(np.uint8)
    return words, np.ascontiguousarray(byte.astype(np.uint8).reshape(k // 512, 16, n))


def unpack_weight(words, scales):
    g, p, n, _ = words.shape
    vals = np.ascontiguousarray(words).view(ml_dtypes.float8_e4m3fn).astype(np.float64) * np.repeat(np.exp2(scales.astype(np.float64) - 127.0), 8, axis=1)[..., None]
    return vals.transpose(0, 1, 3, 2).reshape(g * 512, n)


K, T, S, H = 512, 2048, 512, 512


def setup_inputs():
    n = np.random.standard_normal
    s = mx_kscale(K)[:, None]
    u = mx_kscale(H)
    packed_xT = pack_weight(n((K, T)) * s)
    return {
        "x_words": packed_xT[0],
        "x_scales": packed_xT[1],
        "w1": (n((K, H)) / np.sqrt(K) / s).astype(np.float32),
        "gn": (np.random.uniform(0.5, 1.5, (H, 1)) * u[:, None]).astype(np.float32),
        "w2": (n((H, H)) / np.sqrt(H) / u[:, None]).astype(np.float32),
        "w3": (n((H, H)) / np.sqrt(H) / u[:, None]).astype(np.float32),
        "offs": striped8(np.stack([np.random.permutation(T)[:S] for _ in range(8)])),
        "pair": striped8(np.stack([np.random.permutation(S) for _ in range(8)])),
    }


def reference(x_words, x_scales, w1, gn, w2, w3, offs, pair):
    xq = unpack_weight(x_words, x_scales)[np.arange(K)[:, None], runs(offs, K)]
    y = mxq(f64(w1), 0, "e4m3").T @ xq
    z = f64(gn) * y
    x1 = y + y * (0.5 * ((mxq(f64(w2), 0, "e4m3").T @ mxq(z, 0, "e4m3"))))
    z2 = f64(gn) * (x1[np.arange(H)[:, None], runs(pair, H)])
    return x1 + y * (0.5 * ((mxq(f64(w3), 0, "e4m3").T @ mxq(z2, 0, "e4m3"))))

@@ -1,0 +1,221 @@
+from contextlib import ExitStack
+
+import concourse.mybir as mybir
+
+K, T, S, H = 512, 2048, 512, 512
+FLOPS = 3 * 2 * 512 * 512 * 512
+
+F32 = mybir.dt.float32
+BF16 = mybir.dt.bfloat16
+I32 = mybir.dt.int32
+U32 = mybir.dt.uint32
+U16 = mybir.dt.uint16
+U8 = mybir.dt.uint8
+FP8X4 = mybir.dt.float8_e4m3fn_x4
+MULT = mybir.AluOpType.mult
+ADD = mybir.AluOpType.add
+COPY = mybir.ActivationFunctionType.Copy
+
+P = 128
+PACK = 4
+HALF = S // 2
+LIST_ROWS = 16
+
+
+def offsets(lists, start, count):
+    return lists[:, start // LIST_ROWS : (start + count) // LIST_ROWS]
+
+
+def deal_weight(copy, grouped, raw, m0, m1):
+    copy(
+        out=grouped[:, :, m0:m1, :].rearrange("p t m j -> p m t j"),
+        in_=raw[:].rearrange("p j (m t) -> p m t j", t=PACK)[:, m0:m1],
+    )
+
+
+def tile_picked_dcn2_none_p_kernel(tc, x_words, x_scales, w1, gn, w2, w3, offs, pair, out):
+    nc = tc.nc
+    out_rows = out.rearrange("(p t) j -> p t j", t=PACK)
+
+    with ExitStack() as ctx:
+        keep = ctx.enter_context(tc.tile_pool(name="keep", bufs=1))
+        psum = ctx.enter_context(tc.psum_pool(name="psum", bufs=1))
+
+        def quantize(codes, scales, values):
+            nc.vector.quantize_mx(out=codes.bitcast(FP8X4), scales=scales, in_=values)
+
+        def product(acc, weight, t, codes, scales, start, stop):
+            cols = slice(t * P, (t + 1) * P)
+            nc.tensor.matmul_mx(
+                out=acc,
+                lhsT=weight[0][:, cols].bitcast(FP8X4),
+                lhsT_scale=weight[1][:, cols],
+                rhs=codes.bitcast(FP8X4),
+                rhs_scale=scales,
+                start=start,
+                stop=stop,
+            )
+
+        def mx_tiles(name):
+            return (
+                keep.tile([P, S], U32, name=name + "_codes", align_bytes=64),
+                keep.tile([P, S], U8, name=name + "_scales", align_bytes=64),
+            )
+
+        scale_table = keep.tile([P, T], U8, name="scale_table")
+        nc.vector.memset(scale_table[:].bitcast(I32), 0)
+        offs_sb = keep.tile([P, S // LIST_ROWS], U16, name="offs_sb")
+        nc.sync.dma_start(offs_sb[:], offs)
+        pair_sb = keep.tile([P, S // LIST_ROWS], U16, name="pair_sb")
+        nc.sync.dma_start(pair_sb[:], pair)
+        gain = keep.tile([P, PACK], F32, name="gain")
+        nc.sync.dma_start(out=gain[:], in_=gn.rearrange("(p t) o -> p (t o)", t=PACK))
+        for r in range(2):
+            nc.sync.dma_start(out=scale_table[r:P:16, :].bitcast(I32), in_=x_scales[0][r:16:2, :].bitcast(I32))
+        w1_raw = keep.tile([P, PACK, H], F32, name="w1_raw", tag="raw13")
+        nc.sync.dma_start(out=w1_raw[:], in_=w1.rearrange("(p j) c -> p j c", j=PACK))
+        word_table = keep.tile([P, T], I32, name="word_table")
+        nc.sync.dma_start(out=word_table[:], in_=x_words[0].rearrange("p n t -> p (n t)").bitcast(I32))
+        w2_rows = w2.rearrange("(p j) c -> p j c", j=PACK)
+        w2_raw = []
+        for h in range(2):
+            part = keep.tile([P, PACK, HALF], F32, name="w2_raw%d" % h)
+            nc.sync.dma_start(out=part[:], in_=w2_rows[:, :, h * HALF : (h + 1) * HALF])
+            w2_raw.append(part)
+
+        half_gain = keep.tile([P, PACK], F32, name="half_gain")
+        nc.scalar.activation(half_gain[:], gain[:], COPY, scale=0.5)
+
+        picked_scales = keep.tile([P, S], U8, name="picked_scales")
+        nc.vector.tensor_copy(picked_scales[:], scale_table[:].indirect(offs_sb[:]))
+        x_scale_plane = keep.tile([P, S], U8, name="x_scale_plane", align_bytes=64)
+        nc.vector.tensor_copy(x_scale_plane[:].bitcast(I32), picked_scales[:].bitcast(I32))
+        for r in range(2):
+            nc.scalar.dma_start(
+                out=x_scale_plane[2 + r : P : 32, :].bitcast(I32), in_=picked_scales[16 + r : P : 32, :].bitcast(I32)
+            )
+
+        w1_grouped = keep.tile([P, PACK, P, PACK], BF16, name="w1_grouped", align_bytes=64)
+        deal_weight(nc.vector.tensor_copy, w1_grouped, w1_raw, 0, 96)
+        deal_weight(nc.scalar.copy, w1_grouped, w1_raw, 96, P)
+        w1q = mx_tiles("w1")
+        quantize(w1q[0][:], w1q[1][:], w1_grouped[:].rearrange("p t m j -> p (t m j)"))
+
+        w3_raw = keep.tile([P, PACK, H], F32, name="w3_raw", tag="raw13")
+        nc.sync.dma_start(out=w3_raw[:], in_=w3.rearrange("(p j) c -> p j c", j=PACK))
+
+        half_z = keep.tile([P, PACK, S], F32, name="half_z")
+        half_y = keep.tile([P, PACK, S], F32, name="half_y")
+        zq = mx_tiles("z")
+        w2_grouped = keep.tile([P, PACK, P, PACK], BF16, name="w2_grouped", align_bytes=64)
+        y_banks = {}
+        for h in range(2):
+            cols = slice(h * HALF, (h + 1) * HALF)
+            picked_words = keep.tile([P, HALF], U32, name="picked_words%d" % h, align_bytes=64)
+            nc.vector.tensor_copy(picked_words[:], word_table[:].bitcast(U32).indirect(offsets(offs_sb, h * HALF, HALF)))
+            for u in range(2):
+                bank = psum.tile([P, 2, HALF], F32, name="y%d%d" % (h, u), tag="bank%d" % (2 * h + u))
+                y_banks[h, u] = bank
+                for v in range(2):
+                    product(bank[:, v, :], w1q, 2 * u + v, picked_words[:], x_scale_plane[:, cols], True, True)
+                for v in range(2):
+                    t = 2 * u + v
+                    nc.scalar.activation(half_z[:, t, cols], bank[:, v, :], COPY, scale=half_gain[:, t : t + 1])
+        for h in range(2):
+            nc.vector.tensor_copy(
+                out=w2_grouped[:, :, 64 * h : 64 * h + 64, :].rearrange("p t m j -> p m t j"),
+                in_=w2_raw[h][:].rearrange("p j (m t) -> p m t j", t=PACK),
+            )
+        w2q = mx_tiles("w2")
+        quantize(w2q[0][:], w2q[1][:], w2_grouped[:].rearrange("p t m j -> p (t m j)"))
+        crossed = [keep.tile([P, S], F32, name="crossed%d" % t) for t in range(PACK)]
+        m2_banks = {}
+        for h in range(2):
+            cols = slice(h * HALF, (h + 1) * HALF)
+            z_grouped = keep.tile([P, HALF, PACK], BF16, name="z_grouped%d" % h, align_bytes=64)
+            nc.vector.tensor_scalar(
+                z_grouped[:].rearrange("p (c i) t -> p c t i", i=4),
+                half_z[:, :, cols].rearrange("p t (c i) -> p c t i", i=4),
+                2.0,
+                None,
+                MULT,
+            )
+            quantize(zq[0][:, cols], zq[1][:, cols], z_grouped[:].rearrange("p n t -> p (n t)"))
+            for u in range(2):
+                bank = psum.tile([P, 2, HALF], F32, name="m2_%d%d" % (h, u), tag="bank%d" % (4 + 2 * h + u))
+                m2_banks[h, u] = bank
+                for v in range(2):
+                    product(bank[:, v, :], w2q, 2 * u + v, zq[0][:, cols], zq[1][:, cols], True, True)
+
+        for h in range(2):
+            cols = slice(h * HALF, (h + 1) * HALF)
+            for t in range(PACK):
+                nc.vector.scalar_tensor_tensor(
+                    crossed[t][:, cols], m2_banks[h, t // 2][:, t % 2, :], 2.0, half_z[:, t, cols], ADD, MULT
+                )
+        for h in range(2):
+            for u in range(2):
+                nc.scalar.activation(
+                    half_y[:, 2 * u : 2 * u + 2, h * HALF : (h + 1) * HALF], y_banks[h, u][:], COPY, scale=0.5
+                )
+        m2_kept = keep.tile([P, 2, HALF], F32, name="m2_kept")
+        nc.scalar.copy(out=m2_kept[:], in_=m2_banks[0, 0][:])
+
+        w3_grouped = keep.tile([P, PACK, P, PACK], BF16, name="w3_grouped", align_bytes=64)
+        deal_weight(nc.scalar.copy, w3_grouped, w3_raw, 0, P)
+        w3q = mx_tiles("w3")
+        quantize(w3q[0][:], w3q[1][:], w3_grouped[:].rearrange("p t m j -> p (t m j)"))
+
+        z2q = mx_tiles("z2")
+        chunks = [(0, 256), (256, 128), (384, 128)]
+        grouped = {}
+
+        def fetch(c):
+            start, width = chunks[c]
+            planes = keep.tile(
+                [P, PACK, width], BF16, name="planes%d" % c, tag="stage%d" % (0 if c == 2 else 3 + c), align_bytes=64
+            )
+            for t in range(PACK):
+                nc.vector.tensor_copy(planes[:, t, :], crossed[t][:].indirect(offsets(pair_sb, start, width)))
+            grouped[c] = keep.tile([P, width, PACK], BF16, name="z2_grouped%d" % c, tag="stage%d" % c if c != 2 else "stage2", align_bytes=64)
+            nc.scalar.copy(
+                out=grouped[c][:].rearrange("p (c i) t -> p c t i", i=4),
+                in_=planes[:].rearrange("p t (c i) -> p c t i", i=4),
+            )
+
+        banks = []
+
+        def multiply(c):
+            start, width = chunks[c]
+            cols = slice(start, start + width)
+            quantize(z2q[0][:, cols], z2q[1][:, cols], grouped[c][:].rearrange("p n t -> p (n t)"))
+            per_bank = S // width
+            for t0 in range(0, PACK, per_bank):
+                bank = psum.tile([P, per_bank, width], F32, name="m3_%d_%d" % (c, t0), tag="bank%d" % len(banks))
+                again = len(banks) > 0
+                for v in range(per_bank):
+                    if again:
+                        product(bank[:, v, :], w2q, t0 + v, zq[0][:, cols], zq[1][:, cols], True, False)
+                    product(bank[:, v, :], w3q, t0 + v, z2q[0][:, cols], z2q[1][:, cols], not again, True)
+                banks.append((bank, again, t0, per_bank, cols, width))
+
+        def finish(b):
+            bank, again, t0, per_bank, cols, width = banks[b]
+            result = keep.tile([P, per_bank, width], F32, name="result%d" % b)
+            y_part = half_y[:, t0 : t0 + per_bank, cols]
+            if again:
+                nc.vector.scalar_tensor_tensor(result[:], bank[:], 2.0, y_part, ADD, MULT)
+            else:
+                both = keep.tile([P, per_bank, width], F32, name="both")
+                nc.vector.scalar_tensor_tensor(both[:], bank[:], 2.0, m2_kept[:], ADD, ADD)
+                nc.vector.tensor_tensor(result[:], both[:], y_part, MULT)
+            nc.sync.dma_start(out=out_rows[:, t0 : t0 + per_bank, cols], in_=result[:])
+
+        fetch(0)
+        fetch(1)
+        multiply(0)
+        fetch(2)
+        multiply(1)
+        multiply(2)
+        for b in range(4):
+            finish(b)

@@ -62,42 +62,40 @@ def tile_picked_dcn2_none_p_kernel(tc, x_words, x_scales, w1, gn, w2, w3, offs, 
                 keep.tile([P, S], U8, name=name + "_scales", align_bytes=64),
             )
 
-        scale_table = keep.tile([P, T], U8, name="scale_table")
+        scale_table = keep.tile([P, T], U8, name="scale_table", tag="raw2")
         nc.vector.memset(scale_table[:].bitcast(I32), 0)
         offs_sb = keep.tile([P, S // LIST_ROWS], U16, name="offs_sb")
         nc.sync.dma_start(offs_sb[:], offs)
-        pair_sb = keep.tile([P, S // LIST_ROWS], U16, name="pair_sb")
-        nc.sync.dma_start(pair_sb[:], pair)
         gain = keep.tile([P, PACK], F32, name="gain")
         nc.sync.dma_start(out=gain[:], in_=gn.rearrange("(p t) o -> p (t o)", t=PACK))
-        for r in range(2):
-            nc.sync.dma_start(out=scale_table[r:P:16, :].bitcast(I32), in_=x_scales[0][r:16:2, :].bitcast(I32))
+        w1_rows = w1.rearrange("(p j) c -> p j c", j=PACK)
         w1_raw = keep.tile([P, PACK, H], F32, name="w1_raw", tag="raw13")
-        nc.sync.dma_start(out=w1_raw[:], in_=w1.rearrange("(p j) c -> p j c", j=PACK))
+        nc.sync.dma_start(out=w1_raw[:, 0:2], in_=w1_rows[:, 0:2])
+        nc.sync.dma_start(out=scale_table[0:P:8, :].bitcast(I32), in_=x_scales[0].bitcast(I32))
+        nc.sync.dma_start(out=w1_raw[:, 2:4], in_=w1_rows[:, 2:4])
         word_table = keep.tile([P, T], I32, name="word_table")
         nc.sync.dma_start(out=word_table[:], in_=x_words[0].rearrange("p n t -> p (n t)").bitcast(I32))
-        w2_rows = w2.rearrange("(p j) c -> p j c", j=PACK)
-        w2_raw = []
-        for h in range(2):
-            part = keep.tile([P, PACK, HALF], F32, name="w2_raw%d" % h)
-            nc.sync.dma_start(out=part[:], in_=w2_rows[:, :, h * HALF : (h + 1) * HALF])
-            w2_raw.append(part)
+        pair_sb = keep.tile([P, S // LIST_ROWS], U16, name="pair_sb")
+        nc.sync.dma_start(pair_sb[:], pair)
 
         half_gain = keep.tile([P, PACK], F32, name="half_gain")
         nc.scalar.activation(half_gain[:], gain[:], COPY, scale=0.5)
-
         picked_scales = keep.tile([P, S], U8, name="picked_scales")
         nc.vector.tensor_copy(picked_scales[:], scale_table[:].indirect(offs_sb[:]))
         x_scale_plane = keep.tile([P, S], U8, name="x_scale_plane", align_bytes=64)
-        nc.vector.tensor_copy(x_scale_plane[:].bitcast(I32), picked_scales[:].bitcast(I32))
-        for r in range(2):
-            nc.scalar.dma_start(
-                out=x_scale_plane[2 + r : P : 32, :].bitcast(I32), in_=picked_scales[16 + r : P : 32, :].bitcast(I32)
+        nc.vector.memset(x_scale_plane[:].bitcast(I32), 0)
+        for r in range(4):
+            nc.sync.dma_start(
+                out=x_scale_plane[r:P:32, :].bitcast(I32), in_=picked_scales[8 * r : P : 32, :].bitcast(I32)
             )
+        w2_rows = w2.rearrange("(p j) c -> p j c", j=PACK)
+        w2_raw = keep.tile([P, 2, PACK, HALF], F32, name="w2_raw", tag="raw2")
+        for h in range(2):
+            nc.sync.dma_start(out=w2_raw[:, h], in_=w2_rows[:, :, h * HALF : (h + 1) * HALF])
 
         w1_grouped = keep.tile([P, PACK, P, PACK], BF16, name="w1_grouped", align_bytes=64)
-        deal_weight(nc.vector.tensor_copy, w1_grouped, w1_raw, 0, 96)
-        deal_weight(nc.scalar.copy, w1_grouped, w1_raw, 96, P)
+        deal_weight(nc.vector.tensor_copy, w1_grouped, w1_raw, 0, 88)
+        deal_weight(nc.scalar.copy, w1_grouped, w1_raw, 88, P)
         w1q = mx_tiles("w1")
         quantize(w1q[0][:], w1q[1][:], w1_grouped[:].rearrange("p t m j -> p (t m j)"))
 
@@ -124,45 +122,66 @@ def tile_picked_dcn2_none_p_kernel(tc, x_words, x_scales, w1, gn, w2, w3, offs, 
         for h in range(2):
             nc.vector.tensor_copy(
                 out=w2_grouped[:, :, 64 * h : 64 * h + 64, :].rearrange("p t m j -> p m t j"),
-                in_=w2_raw[h][:].rearrange("p j (m t) -> p m t j", t=PACK),
+                in_=w2_raw[:, h].rearrange("p j (m t) -> p m t j", t=PACK),
             )
         w2q = mx_tiles("w2")
-        quantize(w2q[0][:], w2q[1][:], w2_grouped[:].rearrange("p t m j -> p (t m j)"))
         crossed = [keep.tile([P, S], F32, name="crossed%d" % t) for t in range(PACK)]
         m2_banks = {}
-        for h in range(2):
+        z_grouped = {}
+
+        def group_z(h):
             cols = slice(h * HALF, (h + 1) * HALF)
-            z_grouped = keep.tile([P, HALF, PACK], BF16, name="z_grouped%d" % h, align_bytes=64)
+            z_grouped[h] = keep.tile([P, HALF, PACK], BF16, name="z_grouped%d" % h, align_bytes=64)
             nc.vector.tensor_scalar(
-                z_grouped[:].rearrange("p (c i) t -> p c t i", i=4),
+                z_grouped[h][:].rearrange("p (c i) t -> p c t i", i=4),
                 half_z[:, :, cols].rearrange("p t (c i) -> p c t i", i=4),
                 2.0,
                 None,
                 MULT,
             )
-            quantize(zq[0][:, cols], zq[1][:, cols], z_grouped[:].rearrange("p n t -> p (n t)"))
-            for u in range(2):
+
+        def first_product(h):
+            cols = slice(h * HALF, (h + 1) * HALF)
+            quantize(zq[0][:, cols], zq[1][:, cols], z_grouped[h][:].rearrange("p n t -> p (n t)"))
+            for u in (1, 0):
                 bank = psum.tile([P, 2, HALF], F32, name="m2_%d%d" % (h, u), tag="bank%d" % (4 + 2 * h + u))
                 m2_banks[h, u] = bank
-                for v in range(2):
+                for v in (1, 0):
                     product(bank[:, v, :], w2q, 2 * u + v, zq[0][:, cols], zq[1][:, cols], True, True)
 
-        for h in range(2):
+        def cross(h, t):
             cols = slice(h * HALF, (h + 1) * HALF)
-            for t in range(PACK):
-                nc.vector.scalar_tensor_tensor(
-                    crossed[t][:, cols], m2_banks[h, t // 2][:, t % 2, :], 2.0, half_z[:, t, cols], ADD, MULT
-                )
+            nc.vector.scalar_tensor_tensor(
+                crossed[t][:, cols], m2_banks[h, t // 2][:, t % 2, :], 2.0, half_z[:, t, cols], ADD, MULT
+            )
+
+        m2_kept = keep.tile([P, S], F32, name="m2_kept")
+
+        def keep_m2(h):
+            nc.scalar.activation(m2_kept[:, h * HALF : (h + 1) * HALF], m2_banks[h, 1][:, 1, :], COPY, bias=2.0)
+
+        group_z(0)
+        quantize(w2q[0][:], w2q[1][:], w2_grouped[:].rearrange("p t m j -> p (t m j)"))
+        first_product(0)
+        keep_m2(0)
+        group_z(1)
+        cross(0, 0)
+        first_product(1)
+        keep_m2(1)
+        nc.gpsimd.tensor_tensor(crossed[3][:], m2_kept[:], half_z[:, 3, :], MULT)
+        for t in range(1, 3):
+            cross(0, t)
+        for t in range(3):
+            cross(1, t)
         for h in range(2):
             for u in range(2):
                 nc.scalar.activation(
                     half_y[:, 2 * u : 2 * u + 2, h * HALF : (h + 1) * HALF], y_banks[h, u][:], COPY, scale=0.5
                 )
-        m2_kept = keep.tile([P, 2, HALF], F32, name="m2_kept")
-        nc.scalar.copy(out=m2_kept[:], in_=m2_banks[0, 0][:])
 
         w3_grouped = keep.tile([P, PACK, P, PACK], BF16, name="w3_grouped", align_bytes=64)
-        deal_weight(nc.scalar.copy, w3_grouped, w3_raw, 0, P)
+        for m0 in range(0, P, 32):
+            deal_weight(nc.scalar.copy, w3_grouped, w3_raw, m0, m0 + 32)
         w3q = mx_tiles("w3")
         quantize(w3q[0][:], w3q[1][:], w3_grouped[:].rearrange("p t m j -> p (t m j)"))
 
@@ -192,23 +211,23 @@ def tile_picked_dcn2_none_p_kernel(tc, x_words, x_scales, w1, gn, w2, w3, offs, 
             per_bank = S // width
             for t0 in range(0, PACK, per_bank):
                 bank = psum.tile([P, per_bank, width], F32, name="m3_%d_%d" % (c, t0), tag="bank%d" % len(banks))
-                again = len(banks) > 0
-                for v in range(per_bank):
+                for v in reversed(range(per_bank)):
+                    again = t0 + v != 3
                     if again:
                         product(bank[:, v, :], w2q, t0 + v, zq[0][:, cols], zq[1][:, cols], True, False)
                     product(bank[:, v, :], w3q, t0 + v, z2q[0][:, cols], z2q[1][:, cols], not again, True)
-                banks.append((bank, again, t0, per_bank, cols, width))
+                banks.append((bank, t0, per_bank, cols, width))
 
         def finish(b):
-            bank, again, t0, per_bank, cols, width = banks[b]
+            bank, t0, per_bank, cols, width = banks[b]
             result = keep.tile([P, per_bank, width], F32, name="result%d" % b)
-            y_part = half_y[:, t0 : t0 + per_bank, cols]
-            if again:
-                nc.vector.scalar_tensor_tensor(result[:], bank[:], 2.0, y_part, ADD, MULT)
-            else:
-                both = keep.tile([P, per_bank, width], F32, name="both")
-                nc.vector.scalar_tensor_tensor(both[:], bank[:], 2.0, m2_kept[:], ADD, ADD)
-                nc.vector.tensor_tensor(result[:], both[:], y_part, MULT)
+            n = per_bank
+            if t0 + per_bank == PACK:
+                n = per_bank - 1
+                both = keep.tile([P, width], F32, name="both%d" % b)
+                nc.vector.tensor_tensor(both[:], bank[:, n, :], m2_kept[:, cols], ADD)
+                nc.gpsimd.tensor_tensor(result[:, n, :], both[:], half_y[:, 3, cols], MULT)
+            nc.vector.scalar_tensor_tensor(result[:, 0:n], bank[:, 0:n], 2.0, half_y[:, t0 : t0 + n, cols], ADD, MULT)
             nc.sync.dma_start(out=out_rows[:, t0 : t0 + per_bank, cols], in_=result[:])
 
         fetch(0)

@@ -119,11 +119,13 @@ def tile_picked_dcn2_none_p_kernel(tc, x_words, x_scales, w1, gn, w2, w3, offs, 
                 for v in range(2):
                     t = 2 * u + v
                     nc.scalar.activation(half_z[:, t, cols], bank[:, v, :], COPY, scale=half_gain[:, t : t + 1])
-        for h in range(2):
+
+        def deal_w2(h):
             nc.vector.tensor_copy(
                 out=w2_grouped[:, :, 64 * h : 64 * h + 64, :].rearrange("p t m j -> p m t j"),
                 in_=w2_raw[:, h].rearrange("p j (m t) -> p m t j", t=PACK),
             )
+
         w2q = mx_tiles("w2")
         crossed = [keep.tile([P, S], F32, name="crossed%d" % t) for t in range(PACK)]
         m2_banks = {}
@@ -140,10 +142,13 @@ def tile_picked_dcn2_none_p_kernel(tc, x_words, x_scales, w1, gn, w2, w3, offs, 
                 MULT,
             )
 
-        def first_product(h):
+        def quantize_z(h):
             cols = slice(h * HALF, (h + 1) * HALF)
             quantize(zq[0][:, cols], zq[1][:, cols], z_grouped[h][:].rearrange("p n t -> p (n t)"))
-            for u in (1, 0):
+
+        def first_product(h):
+            cols = slice(h * HALF, (h + 1) * HALF)
+            for u in (h, 1 - h):
                 bank = psum.tile([P, 2, HALF], F32, name="m2_%d%d" % (h, u), tag="bank%d" % (4 + 2 * h + u))
                 m2_banks[h, u] = bank
                 for v in (1, 0):
@@ -160,12 +165,16 @@ def tile_picked_dcn2_none_p_kernel(tc, x_words, x_scales, w1, gn, w2, w3, offs, 
         def keep_m2(h):
             nc.scalar.activation(m2_kept[:, h * HALF : (h + 1) * HALF], m2_banks[h, 1][:, 1, :], COPY, bias=2.0)
 
+        deal_w2(0)
         group_z(0)
+        deal_w2(1)
+        quantize_z(0)
         quantize(w2q[0][:], w2q[1][:], w2_grouped[:].rearrange("p t m j -> p (t m j)"))
         first_product(0)
         keep_m2(0)
         group_z(1)
         cross(0, 0)
+        quantize_z(1)
         first_product(1)
         keep_m2(1)
         nc.gpsimd.tensor_tensor(crossed[3][:], m2_kept[:], half_z[:, 3, :], MULT)
@@ -202,33 +211,50 @@ def tile_picked_dcn2_none_p_kernel(tc, x_words, x_scales, w1, gn, w2, w3, offs, 
                 in_=planes[:].rearrange("p t (c i) -> p c t i", i=4),
             )
 
-        banks = []
+        layout = [[(0, 1), (3, 2)], [(3, 0, 1, 2)], [(3,), (0,), (1,), (2,)]]
+        banks = {}
 
         def multiply(c):
             start, width = chunks[c]
             cols = slice(start, start + width)
             quantize(z2q[0][:, cols], z2q[1][:, cols], grouped[c][:].rearrange("p n t -> p (n t)"))
-            per_bank = S // width
-            for t0 in range(0, PACK, per_bank):
-                bank = psum.tile([P, per_bank, width], F32, name="m3_%d_%d" % (c, t0), tag="bank%d" % len(banks))
-                for v in reversed(range(per_bank)):
-                    again = t0 + v != 3
+            for tiles in layout[c]:
+                first = min(tiles)
+                bank = psum.tile([P, len(tiles), width], F32, name="m3_%d_%d" % (c, first), tag="bank%d" % len(banks))
+                banks[c, first] = bank
+                for t in tiles:
+                    again = t != 3
                     if again:
-                        product(bank[:, v, :], w2q, t0 + v, zq[0][:, cols], zq[1][:, cols], True, False)
-                    product(bank[:, v, :], w3q, t0 + v, z2q[0][:, cols], z2q[1][:, cols], not again, True)
-                banks.append((bank, t0, per_bank, cols, width))
+                        product(bank[:, t - first, :], w2q, t, zq[0][:, cols], zq[1][:, cols], True, False)
+                    product(bank[:, t - first, :], w3q, t, z2q[0][:, cols], z2q[1][:, cols], not again, True)
 
-        def finish(b):
-            bank, t0, per_bank, cols, width = banks[b]
-            result = keep.tile([P, per_bank, width], F32, name="result%d" % b)
-            n = per_bank
-            if t0 + per_bank == PACK:
-                n = per_bank - 1
-                both = keep.tile([P, width], F32, name="both%d" % b)
-                nc.vector.tensor_tensor(both[:], bank[:, n, :], m2_kept[:, cols], ADD)
-                nc.gpsimd.tensor_tensor(result[:, n, :], both[:], half_y[:, 3, cols], MULT)
-            nc.vector.scalar_tensor_tensor(result[:, 0:n], bank[:, 0:n], 2.0, half_y[:, t0 : t0 + n, cols], ADD, MULT)
-            nc.sync.dma_start(out=out_rows[:, t0 : t0 + per_bank, cols], in_=result[:])
+        def finish(c, stores):
+            start, width = chunks[c]
+            cols = slice(start, start + width)
+            results = {}
+            for t0, t1, queue in stores:
+                result = keep.tile([P, t1 - t0, width], F32, name="result%d_%d" % (c, t0))
+                for t in range(t0, t1):
+                    results[t] = (result, t0)
+            last = [tiles for tiles in layout[c] if 3 in tiles][0]
+            both = keep.tile([P, width], F32, name="both%d" % c)
+            nc.vector.tensor_tensor(both[:], banks[c, min(last)][:, 3 - min(last), :], m2_kept[:, cols], ADD)
+            nc.gpsimd.tensor_tensor(results[3][0][:, 3 - results[3][1], :], both[:], half_y[:, 3, cols], MULT)
+            for tiles in layout[c]:
+                first = min(tiles)
+                n = len([t for t in tiles if t != 3])
+                if n:
+                    result, t0 = results[first]
+                    nc.vector.scalar_tensor_tensor(
+                        result[:, first - t0 : first - t0 + n],
+                        banks[c, first][:, 0:n],
+                        2.0,
+                        half_y[:, first : first + n, cols],
+                        ADD,
+                        MULT,
+                    )
+            for t0, t1, queue in stores:
+                queue.dma_start(out=out_rows[:, t0:t1, cols], in_=results[t0][0][:])
 
         fetch(0)
         fetch(1)
@@ -236,5 +262,6 @@ def tile_picked_dcn2_none_p_kernel(tc, x_words, x_scales, w1, gn, w2, w3, offs, 
         fetch(2)
         multiply(1)
         multiply(2)
-        for b in range(4):
-            finish(b)
+        finish(0, [(0, 2, nc.sync), (2, 4, nc.sync)])
+        finish(1, [(0, 4, nc.sync)])
+        finish(2, [(0, 2, nc.scalar), (2, 4, nc.sync)])

@@ -39,6 +39,7 @@ def tile_picked_dcn2_none_p_kernel(tc, x_words, x_scales, w1, gn, w2, w3, offs, 
 
     with ExitStack() as ctx:
         keep = ctx.enter_context(tc.tile_pool(name="keep", bufs=1))
+        reuse = ctx.enter_context(tc.tile_pool(name="reuse", bufs=1))
         psum = ctx.enter_context(tc.psum_pool(name="psum", bufs=1))
 
         def quantize(codes, scales, values):
@@ -127,13 +128,13 @@ def tile_picked_dcn2_none_p_kernel(tc, x_words, x_scales, w1, gn, w2, w3, offs, 
             )
 
         w2q = mx_tiles("w2")
-        crossed = [keep.tile([P, S], F32, name="crossed%d" % t) for t in range(PACK)]
+        crossed = []
         m2_banks = {}
         z_grouped = {}
 
         def group_z(h):
             cols = slice(h * HALF, (h + 1) * HALF)
-            z_grouped[h] = keep.tile([P, HALF, PACK], BF16, name="z_grouped%d" % h, align_bytes=64)
+            z_grouped[h] = reuse.tile([P, HALF, PACK], BF16, name="z_grouped%d" % h, offset=(4096, 1024)[h], align_bytes=64)
             nc.vector.tensor_scalar(
                 z_grouped[h][:].rearrange("p (c i) t -> p c t i", i=4),
                 half_z[:, :, cols].rearrange("p t (c i) -> p c t i", i=4),
@@ -148,7 +149,7 @@ def tile_picked_dcn2_none_p_kernel(tc, x_words, x_scales, w1, gn, w2, w3, offs, 
 
         def first_product(h):
             cols = slice(h * HALF, (h + 1) * HALF)
-            for u in (h, 1 - h):
+            for u in (1, 0):
                 bank = psum.tile([P, 2, HALF], F32, name="m2_%d%d" % (h, u), tag="bank%d" % (4 + 2 * h + u))
                 m2_banks[h, u] = bank
                 for v in (1, 0):
@@ -160,10 +161,11 @@ def tile_picked_dcn2_none_p_kernel(tc, x_words, x_scales, w1, gn, w2, w3, offs, 
                 crossed[t][:, cols], m2_banks[h, t // 2][:, t % 2, :], 2.0, half_z[:, t, cols], ADD, MULT
             )
 
-        m2_kept = keep.tile([P, S], F32, name="m2_kept")
-
-        def keep_m2(h):
-            nc.scalar.activation(m2_kept[:, h * HALF : (h + 1) * HALF], m2_banks[h, 1][:, 1, :], COPY, bias=2.0)
+        def halve_y(h):
+            for u in range(2):
+                nc.scalar.activation(
+                    half_y[:, 2 * u : 2 * u + 2, h * HALF : (h + 1) * HALF], y_banks[h, u][:], COPY, scale=0.5
+                )
 
         deal_w2(0)
         group_z(0)
@@ -171,22 +173,25 @@ def tile_picked_dcn2_none_p_kernel(tc, x_words, x_scales, w1, gn, w2, w3, offs, 
         quantize_z(0)
         quantize(w2q[0][:], w2q[1][:], w2_grouped[:].rearrange("p t m j -> p (t m j)"))
         first_product(0)
-        keep_m2(0)
+        m2_kept0 = keep.tile([P, 2, HALF], F32, name="m2_kept0")
+        nc.scalar.activation(m2_kept0[:], m2_banks[0, 1][:], COPY, bias=2.0)
         group_z(1)
-        cross(0, 0)
         quantize_z(1)
         first_product(1)
-        keep_m2(1)
-        nc.gpsimd.tensor_tensor(crossed[3][:], m2_kept[:], half_z[:, 3, :], MULT)
-        for t in range(1, 3):
+        for t in range(PACK):
+            if t < 2:
+                crossed.append(keep.tile([P, S], F32, name="crossed%d" % t))
+            else:
+                crossed.append(reuse.tile([P, S], F32, name="crossed%d" % t, offset=2048 * (t - 2), align_bytes=64))
+        for t in (2, 3):
+            nc.gpsimd.tensor_tensor(crossed[t][:, 0:HALF], m2_kept0[:, t - 2, :], half_z[:, t, 0:HALF], MULT)
+        for t in range(2):
             cross(0, t)
-        for t in range(3):
+        for t in (2, 3, 0, 1):
             cross(1, t)
-        for h in range(2):
-            for u in range(2):
-                nc.scalar.activation(
-                    half_y[:, 2 * u : 2 * u + 2, h * HALF : (h + 1) * HALF], y_banks[h, u][:], COPY, scale=0.5
-                )
+        m2_kept1 = keep.tile([P, HALF], F32, name="m2_kept1")
+        nc.scalar.activation(m2_kept1[:], m2_banks[1, 1][:, 1, :], COPY, bias=2.0)
+        halve_y(0)
 
         w3_grouped = keep.tile([P, PACK, P, PACK], BF16, name="w3_grouped", align_bytes=64)
         for m0 in range(0, P, 32):
@@ -238,7 +243,7 @@ def tile_picked_dcn2_none_p_kernel(tc, x_words, x_scales, w1, gn, w2, w3, offs, 
                     results[t] = (result, t0)
             last = [tiles for tiles in layout[c] if 3 in tiles][0]
             both = keep.tile([P, width], F32, name="both%d" % c)
-            nc.vector.tensor_tensor(both[:], banks[c, min(last)][:, 3 - min(last), :], m2_kept[:, cols], ADD)
+            nc.vector.tensor_tensor(both[:], banks[c, min(last)][:, 3 - min(last), :], m2_kept0[:, 1, :] if c == 0 else m2_kept1[:, start - HALF : start - HALF + width], ADD)
             nc.gpsimd.tensor_tensor(results[3][0][:, 3 - results[3][1], :], both[:], half_y[:, 3, cols], MULT)
             for tiles in layout[c]:
                 first = min(tiles)
@@ -258,6 +263,7 @@ def tile_picked_dcn2_none_p_kernel(tc, x_words, x_scales, w1, gn, w2, w3, offs, 
 
         fetch(0)
         fetch(1)
+        halve_y(1)
         multiply(0)
         fetch(2)
         multiply(1)

@@ -2,7 +2,7 @@ from contextlib import ExitStack
 
 import concourse.mybir as mybir
 
-K, T, S, H = 512, 2048, 512, 512
+T, S, H = 2048, 512, 512
 FLOPS = 3 * 2 * 512 * 512 * 512
 
 F32 = mybir.dt.float32
@@ -20,17 +20,24 @@ P = 128
 PACK = 4
 HALF = S // 2
 LIST_ROWS = 16
+BLOCK_PARTITIONS = 8
+QUADRANT = 32
+LINE = 4
+
+W1_ON_VECTOR = 88
+W3_PIECE = 32
+LAST = PACK - 1
+
+CHUNKS = ((0, 256), (256, 128), (384, 128))
+BANK_TILES = (((0, 1), (LAST, 2)), ((LAST, 0, 1, 2),), ((LAST,), (0,), (1,), (2,)))
 
 
-def offsets(lists, start, count):
+def entries(lists, start, count):
     return lists[:, start // LIST_ROWS : (start + count) // LIST_ROWS]
 
 
-def deal_weight(copy, grouped, raw, m0, m1):
-    copy(
-        out=grouped[:, :, m0:m1, :].rearrange("p t m j -> p m t j"),
-        in_=raw[:].rearrange("p j (m t) -> p m t j", t=PACK)[:, m0:m1],
-    )
+def deal_weight(copy, grouped, raw):
+    copy(out=grouped.rearrange("p t m j -> p m t j"), in_=raw.rearrange("p j m t -> p m t j"))
 
 
 def tile_picked_dcn2_none_p_kernel(tc, x_words, x_scales, w1, gn, w2, w3, offs, pair, out):
@@ -42,37 +49,43 @@ def tile_picked_dcn2_none_p_kernel(tc, x_words, x_scales, w1, gn, w2, w3, offs, 
         reuse = ctx.enter_context(tc.tile_pool(name="reuse", bufs=1))
         psum = ctx.enter_context(tc.psum_pool(name="psum", bufs=1))
 
-        def quantize(codes, scales, values):
-            nc.vector.quantize_mx(out=codes.bitcast(FP8X4), scales=scales, in_=values)
-
-        def product(acc, weight, t, codes, scales, start, stop):
-            cols = slice(t * P, (t + 1) * P)
-            nc.tensor.matmul_mx(
-                out=acc,
-                lhsT=weight[0][:, cols].bitcast(FP8X4),
-                lhsT_scale=weight[1][:, cols],
-                rhs=codes.bitcast(FP8X4),
-                rhs_scale=scales,
-                start=start,
-                stop=stop,
-            )
-
         def mx_tiles(name):
             return (
                 keep.tile([P, S], U32, name=name + "_codes", align_bytes=64),
                 keep.tile([P, S], U8, name=name + "_scales", align_bytes=64),
             )
 
-        scale_table = keep.tile([P, T], U8, name="scale_table", tag="raw2")
+        def quantize(operand, cols, values):
+            codes, scales = operand
+            nc.vector.quantize_mx(out=codes[:, cols].bitcast(FP8X4), scales=scales[:, cols], in_=values)
+
+        def product(acc, weight, t, codes, scales, start, stop):
+            tile_cols = slice(t * P, (t + 1) * P)
+            nc.tensor.matmul_mx(
+                out=acc,
+                lhsT=weight[0][:, tile_cols].bitcast(FP8X4),
+                lhsT_scale=weight[1][:, tile_cols],
+                rhs=codes.bitcast(FP8X4),
+                rhs_scale=scales,
+                start=start,
+                stop=stop,
+            )
+
+        def half_cols(h):
+            return slice(h * HALF, (h + 1) * HALF)
+
+        every_col = slice(0, S)
+
+        scale_table = keep.tile([P, T], U8, name="scale_table", tag="scales_then_w2")
         nc.vector.memset(scale_table[:].bitcast(I32), 0)
         offs_sb = keep.tile([P, S // LIST_ROWS], U16, name="offs_sb")
         nc.sync.dma_start(offs_sb[:], offs)
         gain = keep.tile([P, PACK], F32, name="gain")
         nc.sync.dma_start(out=gain[:], in_=gn.rearrange("(p t) o -> p (t o)", t=PACK))
         w1_rows = w1.rearrange("(p j) c -> p j c", j=PACK)
-        w1_raw = keep.tile([P, PACK, H], F32, name="w1_raw", tag="raw13")
+        w1_raw = keep.tile([P, PACK, H], F32, name="w1_raw", tag="w1_then_w3")
         nc.sync.dma_start(out=w1_raw[:, 0:2], in_=w1_rows[:, 0:2])
-        nc.sync.dma_start(out=scale_table[0:P:8, :].bitcast(I32), in_=x_scales[0].bitcast(I32))
+        nc.sync.dma_start(out=scale_table[0:P:BLOCK_PARTITIONS, :].bitcast(I32), in_=x_scales[0].bitcast(I32))
         nc.sync.dma_start(out=w1_raw[:, 2:4], in_=w1_rows[:, 2:4])
         word_table = keep.tile([P, T], I32, name="word_table")
         nc.sync.dma_start(out=word_table[:], in_=x_words[0].rearrange("p n t -> p (n t)").bitcast(I32))
@@ -81,26 +94,30 @@ def tile_picked_dcn2_none_p_kernel(tc, x_words, x_scales, w1, gn, w2, w3, offs, 
 
         half_gain = keep.tile([P, PACK], F32, name="half_gain")
         nc.scalar.activation(half_gain[:], gain[:], COPY, scale=0.5)
+
         picked_scales = keep.tile([P, S], U8, name="picked_scales")
         nc.vector.tensor_copy(picked_scales[:], scale_table[:].indirect(offs_sb[:]))
         x_scale_plane = keep.tile([P, S], U8, name="x_scale_plane", align_bytes=64)
         nc.vector.memset(x_scale_plane[:].bitcast(I32), 0)
-        for r in range(4):
+        for r in range(QUADRANT // BLOCK_PARTITIONS):
             nc.sync.dma_start(
-                out=x_scale_plane[r:P:32, :].bitcast(I32), in_=picked_scales[8 * r : P : 32, :].bitcast(I32)
+                out=x_scale_plane[r:P:QUADRANT, :].bitcast(I32),
+                in_=picked_scales[BLOCK_PARTITIONS * r : P : QUADRANT, :].bitcast(I32),
             )
+
         w2_rows = w2.rearrange("(p j) c -> p j c", j=PACK)
-        w2_raw = keep.tile([P, 2, PACK, HALF], F32, name="w2_raw", tag="raw2")
+        w2_raw = keep.tile([P, 2, PACK, HALF], F32, name="w2_raw", tag="scales_then_w2")
         for h in range(2):
-            nc.sync.dma_start(out=w2_raw[:, h], in_=w2_rows[:, :, h * HALF : (h + 1) * HALF])
+            nc.sync.dma_start(out=w2_raw[:, h], in_=w2_rows[:, :, half_cols(h)])
 
         w1_grouped = keep.tile([P, PACK, P, PACK], BF16, name="w1_grouped", align_bytes=64)
-        deal_weight(nc.vector.tensor_copy, w1_grouped, w1_raw, 0, 88)
-        deal_weight(nc.scalar.copy, w1_grouped, w1_raw, 88, P)
+        w1_groups = w1_raw[:].rearrange("p j (m t) -> p j m t", t=PACK)
+        deal_weight(nc.vector.tensor_copy, w1_grouped[:, :, 0:W1_ON_VECTOR], w1_groups[:, :, 0:W1_ON_VECTOR])
+        deal_weight(nc.scalar.copy, w1_grouped[:, :, W1_ON_VECTOR:P], w1_groups[:, :, W1_ON_VECTOR:P])
         w1q = mx_tiles("w1")
-        quantize(w1q[0][:], w1q[1][:], w1_grouped[:].rearrange("p t m j -> p (t m j)"))
+        quantize(w1q, every_col, w1_grouped[:].rearrange("p t m j -> p (t m j)"))
 
-        w3_raw = keep.tile([P, PACK, H], F32, name="w3_raw", tag="raw13")
+        w3_raw = keep.tile([P, PACK, H], F32, name="w3_raw", tag="w1_then_w3")
         nc.sync.dma_start(out=w3_raw[:], in_=w3.rearrange("(p j) c -> p j c", j=PACK))
 
         half_z = keep.tile([P, PACK, S], F32, name="half_z")
@@ -109,165 +126,157 @@ def tile_picked_dcn2_none_p_kernel(tc, x_words, x_scales, w1, gn, w2, w3, offs, 
         w2_grouped = keep.tile([P, PACK, P, PACK], BF16, name="w2_grouped", align_bytes=64)
         y_banks = {}
         for h in range(2):
-            cols = slice(h * HALF, (h + 1) * HALF)
+            cols = half_cols(h)
             picked_words = keep.tile([P, HALF], U32, name="picked_words%d" % h, align_bytes=64)
-            nc.vector.tensor_copy(picked_words[:], word_table[:].bitcast(U32).indirect(offsets(offs_sb, h * HALF, HALF)))
-            for u in range(2):
+            nc.vector.tensor_copy(picked_words[:], word_table[:].bitcast(U32).indirect(entries(offs_sb, h * HALF, HALF)))
+            for u in (1 - h, h):
                 bank = psum.tile([P, 2, HALF], F32, name="y%d%d" % (h, u), tag="bank%d" % (2 * h + u))
+                first_bank = not y_banks
                 y_banks[h, u] = bank
                 for v in range(2):
                     product(bank[:, v, :], w1q, 2 * u + v, picked_words[:], x_scale_plane[:, cols], True, True)
                 for v in range(2):
                     t = 2 * u + v
-                    nc.scalar.activation(half_z[:, t, cols], bank[:, v, :], COPY, scale=half_gain[:, t : t + 1])
-
-        def deal_w2(h):
-            nc.vector.tensor_copy(
-                out=w2_grouped[:, :, 64 * h : 64 * h + 64, :].rearrange("p t m j -> p m t j"),
-                in_=w2_raw[:, h].rearrange("p j (m t) -> p m t j", t=PACK),
-            )
+                    if first_bank:
+                        nc.vector.tensor_scalar(half_z[:, t, cols], bank[:, v, :], half_gain[:, t : t + 1], None, MULT)
+                    else:
+                        nc.scalar.activation(half_z[:, t, cols], bank[:, v, :], COPY, scale=half_gain[:, t : t + 1])
 
         w2q = mx_tiles("w2")
-        crossed = []
         m2_banks = {}
         z_grouped = {}
 
+        window_bytes = S * 4
+        z_grouped_at = (2 * window_bytes, window_bytes // 2)
+
+        def deal_w2(h):
+            groups = slice(h * P // 2, (h + 1) * P // 2)
+            deal_weight(nc.vector.tensor_copy, w2_grouped[:, :, groups], w2_raw[:, h].rearrange("p j (m t) -> p j m t", t=PACK))
+
         def group_z(h):
-            cols = slice(h * HALF, (h + 1) * HALF)
-            z_grouped[h] = reuse.tile([P, HALF, PACK], BF16, name="z_grouped%d" % h, offset=(4096, 1024)[h], align_bytes=64)
+            z_grouped[h] = reuse.tile([P, HALF, PACK], BF16, name="z_grouped%d" % h, offset=z_grouped_at[h], align_bytes=64)
             nc.vector.tensor_scalar(
-                z_grouped[h][:].rearrange("p (c i) t -> p c t i", i=4),
-                half_z[:, :, cols].rearrange("p t (c i) -> p c t i", i=4),
+                z_grouped[h][:].rearrange("p (c i) t -> p c t i", i=LINE),
+                half_z[:, :, half_cols(h)].rearrange("p t (c i) -> p c t i", i=LINE),
                 2.0,
                 None,
                 MULT,
             )
 
         def quantize_z(h):
-            cols = slice(h * HALF, (h + 1) * HALF)
-            quantize(zq[0][:, cols], zq[1][:, cols], z_grouped[h][:].rearrange("p n t -> p (n t)"))
+            quantize(zq, half_cols(h), z_grouped[h][:].rearrange("p n t -> p (n t)"))
 
-        def first_product(h):
-            cols = slice(h * HALF, (h + 1) * HALF)
+        def multiply_w2(h):
+            cols = half_cols(h)
             for u in (1, 0):
                 bank = psum.tile([P, 2, HALF], F32, name="m2_%d%d" % (h, u), tag="bank%d" % (4 + 2 * h + u))
                 m2_banks[h, u] = bank
                 for v in (1, 0):
                     product(bank[:, v, :], w2q, 2 * u + v, zq[0][:, cols], zq[1][:, cols], True, True)
 
-        def cross(h, t):
-            cols = slice(h * HALF, (h + 1) * HALF)
-            nc.vector.scalar_tensor_tensor(
-                crossed[t][:, cols], m2_banks[h, t // 2][:, t % 2, :], 2.0, half_z[:, t, cols], ADD, MULT
-            )
-
         def halve_y(h):
             for u in range(2):
-                nc.scalar.activation(
-                    half_y[:, 2 * u : 2 * u + 2, h * HALF : (h + 1) * HALF], y_banks[h, u][:], COPY, scale=0.5
-                )
+                nc.scalar.activation(half_y[:, 2 * u : 2 * u + 2, half_cols(h)], y_banks[h, u][:], COPY, scale=0.5)
 
         deal_w2(0)
         group_z(0)
         deal_w2(1)
         quantize_z(0)
-        quantize(w2q[0][:], w2q[1][:], w2_grouped[:].rearrange("p t m j -> p (t m j)"))
-        first_product(0)
-        m2_kept0 = keep.tile([P, 2, HALF], F32, name="m2_kept0")
-        nc.scalar.activation(m2_kept0[:], m2_banks[0, 1][:], COPY, bias=2.0)
+        quantize(w2q, every_col, w2_grouped[:].rearrange("p t m j -> p (t m j)"))
+        multiply_w2(0)
+        kept_first = keep.tile([P, 2, HALF], F32, name="kept_first")
+        nc.scalar.activation(kept_first[:], m2_banks[0, 1][:], COPY, bias=2.0)
         group_z(1)
         quantize_z(1)
-        first_product(1)
-        for t in range(PACK):
-            if t < 2:
-                crossed.append(keep.tile([P, S], F32, name="crossed%d" % t))
-            else:
-                crossed.append(reuse.tile([P, S], F32, name="crossed%d" % t, offset=2048 * (t - 2), align_bytes=64))
+        multiply_w2(1)
+
+        windows = [keep.tile([P, S], F32, name="window%d" % t) for t in range(2)]
+        windows = windows + [
+            reuse.tile([P, S], F32, name="window%d" % t, offset=window_bytes * (t - 2), align_bytes=64) for t in (2, 3)
+        ]
         for t in (2, 3):
-            nc.gpsimd.tensor_tensor(crossed[t][:, 0:HALF], m2_kept0[:, t - 2, :], half_z[:, t, 0:HALF], MULT)
-        for t in range(2):
-            cross(0, t)
-        for t in (2, 3, 0, 1):
-            cross(1, t)
-        m2_kept1 = keep.tile([P, HALF], F32, name="m2_kept1")
-        nc.scalar.activation(m2_kept1[:], m2_banks[1, 1][:, 1, :], COPY, bias=2.0)
+            nc.gpsimd.tensor_tensor(windows[t][:, half_cols(0)], kept_first[:, t - 2, :], half_z[:, t, half_cols(0)], MULT)
+        for h, tiles in ((0, (0, 1)), (1, (2, 3, 0, 1))):
+            cols = half_cols(h)
+            for t in tiles:
+                nc.vector.scalar_tensor_tensor(
+                    windows[t][:, cols], m2_banks[h, t // 2][:, t % 2, :], 2.0, half_z[:, t, cols], ADD, MULT
+                )
+        kept_second = keep.tile([P, HALF], F32, name="kept_second")
+        nc.scalar.activation(kept_second[:], m2_banks[1, 1][:, 1, :], COPY, bias=2.0)
         halve_y(0)
 
         w3_grouped = keep.tile([P, PACK, P, PACK], BF16, name="w3_grouped", align_bytes=64)
-        for m0 in range(0, P, 32):
-            deal_weight(nc.scalar.copy, w3_grouped, w3_raw, m0, m0 + 32)
+        w3_groups = w3_raw[:].rearrange("p j (m t) -> p j m t", t=PACK)
+        for m0 in range(0, P, W3_PIECE):
+            deal_weight(nc.scalar.copy, w3_grouped[:, :, m0 : m0 + W3_PIECE], w3_groups[:, :, m0 : m0 + W3_PIECE])
         w3q = mx_tiles("w3")
-        quantize(w3q[0][:], w3q[1][:], w3_grouped[:].rearrange("p t m j -> p (t m j)"))
+        quantize(w3q, every_col, w3_grouped[:].rearrange("p t m j -> p (t m j)"))
 
         z2q = mx_tiles("z2")
-        chunks = [(0, 256), (256, 128), (384, 128)]
-        grouped = {}
+        z2_grouped = {}
+        sum_banks = {}
 
-        def fetch(c):
-            start, width = chunks[c]
-            planes = keep.tile(
-                [P, PACK, width], BF16, name="planes%d" % c, tag="stage%d" % (0 if c == 2 else 3 + c), align_bytes=64
-            )
+        def fetch(c, buffer):
+            start, width = CHUNKS[c]
+            fetched = keep.tile([P, PACK, width], BF16, name="fetched%d" % c, tag=buffer, align_bytes=64)
             for t in range(PACK):
-                nc.vector.tensor_copy(planes[:, t, :], crossed[t][:].indirect(offsets(pair_sb, start, width)))
-            grouped[c] = keep.tile([P, width, PACK], BF16, name="z2_grouped%d" % c, tag="stage%d" % c if c != 2 else "stage2", align_bytes=64)
+                nc.vector.tensor_copy(fetched[:, t, :], windows[t][:].indirect(entries(pair_sb, start, width)))
+            z2_grouped[c] = keep.tile([P, width, PACK], BF16, name="z2_grouped%d" % c, tag="z2_grouped%d" % c, align_bytes=64)
             nc.scalar.copy(
-                out=grouped[c][:].rearrange("p (c i) t -> p c t i", i=4),
-                in_=planes[:].rearrange("p t (c i) -> p c t i", i=4),
+                out=z2_grouped[c][:].rearrange("p (c i) t -> p c t i", i=LINE),
+                in_=fetched[:].rearrange("p t (c i) -> p c t i", i=LINE),
             )
 
-        layout = [[(0, 1), (3, 2)], [(3, 0, 1, 2)], [(3,), (0,), (1,), (2,)]]
-        banks = {}
-
-        def multiply(c):
-            start, width = chunks[c]
+        def multiply_w3(c):
+            start, width = CHUNKS[c]
             cols = slice(start, start + width)
-            quantize(z2q[0][:, cols], z2q[1][:, cols], grouped[c][:].rearrange("p n t -> p (n t)"))
-            for tiles in layout[c]:
+            quantize(z2q, cols, z2_grouped[c][:].rearrange("p n t -> p (n t)"))
+            for tiles in BANK_TILES[c]:
                 first = min(tiles)
-                bank = psum.tile([P, len(tiles), width], F32, name="m3_%d_%d" % (c, first), tag="bank%d" % len(banks))
-                banks[c, first] = bank
+                bank = psum.tile([P, len(tiles), width], F32, name="sum%d_%d" % (c, first), tag="bank%d" % len(sum_banks))
+                sum_banks[c, first] = bank
                 for t in tiles:
-                    again = t != 3
-                    if again:
+                    if t != LAST:
                         product(bank[:, t - first, :], w2q, t, zq[0][:, cols], zq[1][:, cols], True, False)
-                    product(bank[:, t - first, :], w3q, t, z2q[0][:, cols], z2q[1][:, cols], not again, True)
+                    product(bank[:, t - first, :], w3q, t, z2q[0][:, cols], z2q[1][:, cols], t == LAST, True)
 
-        def finish(c, stores):
-            start, width = chunks[c]
+        def finish(c, kept, stores):
+            start, width = CHUNKS[c]
             cols = slice(start, start + width)
             results = {}
             for t0, t1, queue in stores:
                 result = keep.tile([P, t1 - t0, width], F32, name="result%d_%d" % (c, t0))
                 for t in range(t0, t1):
                     results[t] = (result, t0)
-            last = [tiles for tiles in layout[c] if 3 in tiles][0]
-            both = keep.tile([P, width], F32, name="both%d" % c)
-            nc.vector.tensor_tensor(both[:], banks[c, min(last)][:, 3 - min(last), :], m2_kept0[:, 1, :] if c == 0 else m2_kept1[:, start - HALF : start - HALF + width], ADD)
-            nc.gpsimd.tensor_tensor(results[3][0][:, 3 - results[3][1], :], both[:], half_y[:, 3, cols], MULT)
-            for tiles in layout[c]:
+            first = [min(tiles) for tiles in BANK_TILES[c] if LAST in tiles][0]
+            last_sum = keep.tile([P, width], F32, name="last_sum%d" % c)
+            nc.vector.tensor_tensor(last_sum[:], sum_banks[c, first][:, LAST - first, :], kept, ADD)
+            result, t0 = results[LAST]
+            nc.gpsimd.tensor_tensor(result[:, LAST - t0, :], last_sum[:], half_y[:, LAST, cols], MULT)
+            for tiles in BANK_TILES[c]:
                 first = min(tiles)
-                n = len([t for t in tiles if t != 3])
-                if n:
+                count = len([t for t in tiles if t != LAST])
+                if count:
                     result, t0 = results[first]
                     nc.vector.scalar_tensor_tensor(
-                        result[:, first - t0 : first - t0 + n],
-                        banks[c, first][:, 0:n],
+                        result[:, first - t0 : first - t0 + count],
+                        sum_banks[c, first][:, 0:count],
                         2.0,
-                        half_y[:, first : first + n, cols],
+                        half_y[:, first : first + count, cols],
                         ADD,
                         MULT,
                     )
             for t0, t1, queue in stores:
                 queue.dma_start(out=out_rows[:, t0:t1, cols], in_=results[t0][0][:])
 
-        fetch(0)
-        fetch(1)
+        fetch(0, "fetched0")
+        fetch(1, "fetched1")
         halve_y(1)
-        multiply(0)
-        fetch(2)
-        multiply(1)
-        multiply(2)
-        finish(0, [(0, 2, nc.sync), (2, 4, nc.sync)])
-        finish(1, [(0, 4, nc.sync)])
-        finish(2, [(0, 2, nc.scalar), (2, 4, nc.sync)])
+        multiply_w3(0)
+        fetch(2, "z2_grouped0")
+        multiply_w3(1)
+        multiply_w3(2)
+        finish(0, kept_first[:, 1, :], [(0, 2, nc.sync), (2, 4, nc.sync)])
+        finish(1, kept_second[:, 0:P], [(0, 4, nc.sync)])
+        finish(2, kept_second[:, P:HALF], [(0, 2, nc.scalar), (2, 4, nc.sync)])

from contextlib import ExitStack

import concourse.mybir as mybir

T, S, H = 2048, 512, 512
FLOPS = 3 * 2 * 512 * 512 * 512

F32 = mybir.dt.float32
BF16 = mybir.dt.bfloat16
I32 = mybir.dt.int32
U32 = mybir.dt.uint32
U16 = mybir.dt.uint16
U8 = mybir.dt.uint8
FP8X4 = mybir.dt.float8_e4m3fn_x4
MULT = mybir.AluOpType.mult
ADD = mybir.AluOpType.add
COPY = mybir.ActivationFunctionType.Copy

P = 128
PACK = 4
HALF = S // 2
LIST_ROWS = 16
BLOCK_PARTITIONS = 8
QUADRANT = 32
LINE = 4

W1_ON_VECTOR = 88
W3_PIECE = 32
LAST = PACK - 1

CHUNKS = ((0, 256), (256, 128), (384, 128))
BANK_TILES = (((0, 1), (LAST, 2)), ((LAST, 0, 1, 2),), ((LAST,), (0,), (1,), (2,)))


def entries(lists, start, count):
    return lists[:, start // LIST_ROWS : (start + count) // LIST_ROWS]


def deal_weight(copy, grouped, raw):
    copy(out=grouped.rearrange("p t m j -> p m t j"), in_=raw.rearrange("p j m t -> p m t j"))


def tile_picked_dcn2_none_p_kernel(tc, x_words, x_scales, w1, gn, w2, w3, offs, pair, out):
    nc = tc.nc
    out_rows = out.rearrange("(p t) j -> p t j", t=PACK)

    with ExitStack() as ctx:
        keep = ctx.enter_context(tc.tile_pool(name="keep", bufs=1))
        reuse = ctx.enter_context(tc.tile_pool(name="reuse", bufs=1))
        psum = ctx.enter_context(tc.psum_pool(name="psum", bufs=1))

        def mx_tiles(name):
            return (
                keep.tile([P, S], U32, name=name + "_codes", align_bytes=64),
                keep.tile([P, S], U8, name=name + "_scales", align_bytes=64),
            )

        def quantize(operand, cols, values):
            codes, scales = operand
            nc.vector.quantize_mx(out=codes[:, cols].bitcast(FP8X4), scales=scales[:, cols], in_=values)

        def product(acc, weight, t, codes, scales, start, stop):
            tile_cols = slice(t * P, (t + 1) * P)
            nc.tensor.matmul_mx(
                out=acc,
                lhsT=weight[0][:, tile_cols].bitcast(FP8X4),
                lhsT_scale=weight[1][:, tile_cols],
                rhs=codes.bitcast(FP8X4),
                rhs_scale=scales,
                start=start,
                stop=stop,
            )

        def half_cols(h):
            return slice(h * HALF, (h + 1) * HALF)

        every_col = slice(0, S)

        scale_table = keep.tile([P, T], U8, name="scale_table", tag="scales_then_w2")
        nc.vector.memset(scale_table[:].bitcast(I32), 0)
        offs_sb = keep.tile([P, S // LIST_ROWS], U16, name="offs_sb")
        nc.sync.dma_start(offs_sb[:], offs)
        gain = keep.tile([P, PACK], F32, name="gain")
        nc.sync.dma_start(out=gain[:], in_=gn.rearrange("(p t) o -> p (t o)", t=PACK))
        w1_rows = w1.rearrange("(p j) c -> p j c", j=PACK)
        w1_raw = keep.tile([P, PACK, H], F32, name="w1_raw", tag="w1_then_w3")
        nc.sync.dma_start(out=w1_raw[:, 0:2], in_=w1_rows[:, 0:2])
        nc.sync.dma_start(out=scale_table[0:P:BLOCK_PARTITIONS, :].bitcast(I32), in_=x_scales[0].bitcast(I32))
        nc.sync.dma_start(out=w1_raw[:, 2:4], in_=w1_rows[:, 2:4])
        word_table = keep.tile([P, T], I32, name="word_table")
        nc.sync.dma_start(out=word_table[:], in_=x_words[0].rearrange("p n t -> p (n t)").bitcast(I32))
        pair_sb = keep.tile([P, S // LIST_ROWS], U16, name="pair_sb")
        nc.sync.dma_start(pair_sb[:], pair)

        half_gain = keep.tile([P, PACK], F32, name="half_gain")
        nc.scalar.activation(half_gain[:], gain[:], COPY, scale=0.5)

        picked_scales = keep.tile([P, S], U8, name="picked_scales")
        nc.vector.tensor_copy(picked_scales[:], scale_table[:].indirect(offs_sb[:]))
        x_scale_plane = keep.tile([P, S], U8, name="x_scale_plane", align_bytes=64)
        nc.vector.memset(x_scale_plane[:].bitcast(I32), 0)
        for r in range(QUADRANT // BLOCK_PARTITIONS):
            nc.sync.dma_start(
                out=x_scale_plane[r:P:QUADRANT, :].bitcast(I32),
                in_=picked_scales[BLOCK_PARTITIONS * r : P : QUADRANT, :].bitcast(I32),
            )

        w2_rows = w2.rearrange("(p j) c -> p j c", j=PACK)
        w2_raw = keep.tile([P, 2, PACK, HALF], F32, name="w2_raw", tag="scales_then_w2")
        for h in range(2):
            nc.sync.dma_start(out=w2_raw[:, h], in_=w2_rows[:, :, half_cols(h)])

        w1_grouped = keep.tile([P, PACK, P, PACK], BF16, name="w1_grouped", align_bytes=64)
        w1_groups = w1_raw[:].rearrange("p j (m t) -> p j m t", t=PACK)
        deal_weight(nc.vector.tensor_copy, w1_grouped[:, :, 0:W1_ON_VECTOR], w1_groups[:, :, 0:W1_ON_VECTOR])
        deal_weight(nc.scalar.copy, w1_grouped[:, :, W1_ON_VECTOR:P], w1_groups[:, :, W1_ON_VECTOR:P])
        w1q = mx_tiles("w1")
        quantize(w1q, every_col, w1_grouped[:].rearrange("p t m j -> p (t m j)"))

        w3_raw = keep.tile([P, PACK, H], F32, name="w3_raw", tag="w1_then_w3")
        nc.sync.dma_start(out=w3_raw[:], in_=w3.rearrange("(p j) c -> p j c", j=PACK))

        half_z = keep.tile([P, PACK, S], F32, name="half_z")
        half_y = keep.tile([P, PACK, S], F32, name="half_y")
        zq = mx_tiles("z")
        w2_grouped = keep.tile([P, PACK, P, PACK], BF16, name="w2_grouped", align_bytes=64)
        y_banks = {}
        for h in range(2):
            cols = half_cols(h)
            picked_words = keep.tile([P, HALF], U32, name="picked_words%d" % h, align_bytes=64)
            nc.vector.tensor_copy(picked_words[:], word_table[:].bitcast(U32).indirect(entries(offs_sb, h * HALF, HALF)))
            for u in (1 - h, h):
                bank = psum.tile([P, 2, HALF], F32, name="y%d%d" % (h, u), tag="bank%d" % (2 * h + u))
                first_bank = not y_banks
                y_banks[h, u] = bank
                for v in range(2):
                    product(bank[:, v, :], w1q, 2 * u + v, picked_words[:], x_scale_plane[:, cols], True, True)
                for v in range(2):
                    t = 2 * u + v
                    if first_bank:
                        nc.vector.tensor_scalar(half_z[:, t, cols], bank[:, v, :], half_gain[:, t : t + 1], None, MULT)
                    else:
                        nc.scalar.activation(half_z[:, t, cols], bank[:, v, :], COPY, scale=half_gain[:, t : t + 1])

        w2q = mx_tiles("w2")
        m2_banks = {}
        z_grouped = {}

        window_bytes = S * 4
        z_grouped_at = (2 * window_bytes, window_bytes // 2)

        def deal_w2(h):
            groups = slice(h * P // 2, (h + 1) * P // 2)
            deal_weight(nc.vector.tensor_copy, w2_grouped[:, :, groups], w2_raw[:, h].rearrange("p j (m t) -> p j m t", t=PACK))

        def group_z(h):
            z_grouped[h] = reuse.tile([P, HALF, PACK], BF16, name="z_grouped%d" % h, offset=z_grouped_at[h], align_bytes=64)
            nc.vector.tensor_scalar(
                z_grouped[h][:].rearrange("p (c i) t -> p c t i", i=LINE),
                half_z[:, :, half_cols(h)].rearrange("p t (c i) -> p c t i", i=LINE),
                2.0,
                None,
                MULT,
            )

        def quantize_z(h):
            quantize(zq, half_cols(h), z_grouped[h][:].rearrange("p n t -> p (n t)"))

        def multiply_w2(h):
            cols = half_cols(h)
            for u in (1, 0):
                bank = psum.tile([P, 2, HALF], F32, name="m2_%d%d" % (h, u), tag="bank%d" % (4 + 2 * h + u))
                m2_banks[h, u] = bank
                for v in (1, 0):
                    product(bank[:, v, :], w2q, 2 * u + v, zq[0][:, cols], zq[1][:, cols], True, True)

        def halve_y(h):
            for u in range(2):
                nc.scalar.activation(half_y[:, 2 * u : 2 * u + 2, half_cols(h)], y_banks[h, u][:], COPY, scale=0.5)

        deal_w2(0)
        group_z(0)
        deal_w2(1)
        quantize_z(0)
        quantize(w2q, every_col, w2_grouped[:].rearrange("p t m j -> p (t m j)"))
        multiply_w2(0)
        kept_first = keep.tile([P, 2, HALF], F32, name="kept_first")
        nc.scalar.activation(kept_first[:], m2_banks[0, 1][:], COPY, bias=2.0)
        group_z(1)
        quantize_z(1)
        multiply_w2(1)

        windows = [keep.tile([P, S], F32, name="window%d" % t) for t in range(2)]
        windows = windows + [
            reuse.tile([P, S], F32, name="window%d" % t, offset=window_bytes * (t - 2), align_bytes=64) for t in (2, 3)
        ]
        for t in (2, 3):
            nc.gpsimd.tensor_tensor(windows[t][:, half_cols(0)], kept_first[:, t - 2, :], half_z[:, t, half_cols(0)], MULT)
        for h, tiles in ((0, (0, 1)), (1, (2, 3, 0, 1))):
            cols = half_cols(h)
            for t in tiles:
                nc.vector.scalar_tensor_tensor(
                    windows[t][:, cols], m2_banks[h, t // 2][:, t % 2, :], 2.0, half_z[:, t, cols], ADD, MULT
                )
        kept_second = keep.tile([P, HALF], F32, name="kept_second")
        nc.scalar.activation(kept_second[:], m2_banks[1, 1][:, 1, :], COPY, bias=2.0)
        halve_y(0)

        w3_grouped = keep.tile([P, PACK, P, PACK], BF16, name="w3_grouped", align_bytes=64)
        w3_groups = w3_raw[:].rearrange("p j (m t) -> p j m t", t=PACK)
        for m0 in range(0, P, W3_PIECE):
            deal_weight(nc.scalar.copy, w3_grouped[:, :, m0 : m0 + W3_PIECE], w3_groups[:, :, m0 : m0 + W3_PIECE])
        w3q = mx_tiles("w3")
        quantize(w3q, every_col, w3_grouped[:].rearrange("p t m j -> p (t m j)"))

        z2q = mx_tiles("z2")
        z2_grouped = {}
        sum_banks = {}

        def fetch(c, buffer):
            start, width = CHUNKS[c]
            fetched = keep.tile([P, PACK, width], BF16, name="fetched%d" % c, tag=buffer, align_bytes=64)
            for t in range(PACK):
                nc.vector.tensor_copy(fetched[:, t, :], windows[t][:].indirect(entries(pair_sb, start, width)))
            z2_grouped[c] = keep.tile([P, width, PACK], BF16, name="z2_grouped%d" % c, tag="z2_grouped%d" % c, align_bytes=64)
            nc.scalar.copy(
                out=z2_grouped[c][:].rearrange("p (c i) t -> p c t i", i=LINE),
                in_=fetched[:].rearrange("p t (c i) -> p c t i", i=LINE),
            )

        def multiply_w3(c):
            start, width = CHUNKS[c]
            cols = slice(start, start + width)
            quantize(z2q, cols, z2_grouped[c][:].rearrange("p n t -> p (n t)"))
            for tiles in BANK_TILES[c]:
                first = min(tiles)
                bank = psum.tile([P, len(tiles), width], F32, name="sum%d_%d" % (c, first), tag="bank%d" % len(sum_banks))
                sum_banks[c, first] = bank
                for t in tiles:
                    if t != LAST:
                        product(bank[:, t - first, :], w2q, t, zq[0][:, cols], zq[1][:, cols], True, False)
                    product(bank[:, t - first, :], w3q, t, z2q[0][:, cols], z2q[1][:, cols], t == LAST, True)

        def finish(c, kept, stores):
            start, width = CHUNKS[c]
            cols = slice(start, start + width)
            results = {}
            for t0, t1, queue in stores:
                result = keep.tile([P, t1 - t0, width], F32, name="result%d_%d" % (c, t0))
                for t in range(t0, t1):
                    results[t] = (result, t0)
            first = [min(tiles) for tiles in BANK_TILES[c] if LAST in tiles][0]
            last_sum = keep.tile([P, width], F32, name="last_sum%d" % c)
            nc.vector.tensor_tensor(last_sum[:], sum_banks[c, first][:, LAST - first, :], kept, ADD)
            result, t0 = results[LAST]
            nc.gpsimd.tensor_tensor(result[:, LAST - t0, :], last_sum[:], half_y[:, LAST, cols], MULT)
            for tiles in BANK_TILES[c]:
                first = min(tiles)
                count = len([t for t in tiles if t != LAST])
                if count:
                    result, t0 = results[first]
                    nc.vector.scalar_tensor_tensor(
                        result[:, first - t0 : first - t0 + count],
                        sum_banks[c, first][:, 0:count],
                        2.0,
                        half_y[:, first : first + count, cols],
                        ADD,
                        MULT,
                    )
            for t0, t1, queue in stores:
                queue.dma_start(out=out_rows[:, t0:t1, cols], in_=results[t0][0][:])

        fetch(0, "fetched0")
        fetch(1, "fetched1")
        halve_y(1)
        multiply_w3(0)
        fetch(2, "z2_grouped0")
        multiply_w3(1)
        multiply_w3(2)
        finish(0, kept_first[:, 1, :], [(0, 2, nc.sync), (2, 4, nc.sync)])
        finish(1, kept_second[:, 0:P], [(0, 4, nc.sync)])
        finish(2, kept_second[:, P:HALF], [(0, 2, nc.scalar), (2, 4, nc.sync)])
